import numpy as np
import ml_dtypes


def mxq(x, axis, fmt="e4m3"):
    dtype, down = {"e4m3": (ml_dtypes.float8_e4m3fn, 7), "e5m2": (ml_dtypes.float8_e5m2, 14)}[fmt]
    v = np.moveaxis(np.asarray(x, np.float32).astype(ml_dtypes.bfloat16).astype(np.float64), axis, -1)
    blocks = v.reshape(v.shape[:-1] + (-1, 32))
    amax = np.abs(blocks).max(-1, keepdims=True)
    byte = np.maximum(np.where(amax > 0, np.frexp(amax)[1] - 1 + 127, 0) - down, 1)
    scale = np.exp2(byte - 127.0)
    codes = (blocks / scale).astype(np.float32).astype(dtype).astype(np.float64)
    return np.moveaxis((codes * scale).reshape(v.shape), -1, axis)


WIDE = False


def mx_kscale(k):
    if not WIDE:
        return np.ones(k)
    levels = np.array([10, -10, 5, -5, 0])
    if k % 512:
        return np.exp2(np.random.permutation(np.resize(levels, k // 32))).repeat(32)
    a = np.empty((k // 512, 16))
    for p in range(k // 512):
        a[p, :8] = np.random.permutation(np.resize(levels, 8))
        for g in range(8):
            far = levels[np.abs(levels - a[p, g]) >= 10]
            a[p, g + 8] = far[np.random.randint(len(far))]
    return np.exp2(a.ravel()).repeat(32)


def f64(x):
    return np.asarray(x).astype(np.float64)


def striped8(idx):
    return np.asarray(idx).reshape(8, -1, 16).transpose(0, 2, 1).reshape(128, -1).astype(np.uint16)


def unstriped8(offs):
    return offs.reshape(8, 16, -1).transpose(0, 2, 1).reshape(8, -1).astype(np.int64)


def pick8(x, idx, run):
    r = np.arange(len(x))
    return x[r[:, None], idx[r % (8 * run) // run]]


E2M1 = np.array([0.0, 0.5, 1.0, 1.5, 2.0, 3.0, 4.0, 6.0, -0.0, -0.5, -1.0, -1.5, -2.0, -3.0, -4.0, -6.0])


def pack_weight(w, fmt):
    k, n = w.shape
    w = f64(np.asarray(w, np.float32).astype(ml_dtypes.bfloat16)).reshape(k // 32, 32, n)
    amax = np.abs(w).max(1)
    if fmt == "e4m3":
        byte = np.frexp(amax)[1] - 1 + 127 - 7
    else:
        mant, ex = np.frexp(amax / 6.0)
        byte = np.where(mant > 0.5, ex, ex - 1) + 127
    byte = np.clip(np.where(amax > 0, byte, 1), 1, 254)
    scaled = (w * np.exp2(127.0 - byte)[:, None, :]).reshape(k, n).astype(np.float32)
    by_word = np.ascontiguousarray(scaled.reshape(k // 512, 128, 4, n).transpose(0, 1, 3, 2))
    if fmt == "e4m3":
        words = by_word.astype(ml_dtypes.float8_e4m3fn).view(np.uint8)
    else:
        c = by_word.astype(ml_dtypes.float4_e2m1fn).view(np.uint8) & 0xF
        words = (c[..., 0::2] | (c[..., 1::2] << 4)).reshape(k // 512, 128, 2 * n)
    return np.ascontiguousarray(words), np.ascontiguousarray(byte.astype(np.uint8).reshape(k // 512, 16, n))


def unpack_weight(words, scales, fmt):
    g, _, n = scales.shape
    words = np.ascontiguousarray(words).reshape(g, 128, n, -1)
    if fmt == "e4m3":
        vals = words.view(ml_dtypes.float8_e4m3fn).astype(np.float64)
    else:
        nib = np.empty((g, 128, n, 4), np.uint8)
        nib[..., 0::2] = words & 0xF
        nib[..., 1::2] = words >> 4
        vals = E2M1[nib]
    vals = vals * np.repeat(np.exp2(scales.astype(np.float64) - 127.0), 8, axis=1)[..., None]
    return vals.transpose(0, 1, 3, 2).reshape(g * 512, n)


D, T, U, I, J, Q = 512, 1024, 1024, 512, 256, 128


def setup_inputs():
    n = np.random.standard_normal
    idx = np.stack([np.random.permutation(T)[:J] for _ in range(8)])
    idx2 = np.stack([np.random.permutation(U)[:J] for _ in range(8)])
    idx3 = np.stack([np.random.permutation(T)[:I] for _ in range(8)])
    idx4 = np.stack([np.random.permutation(T)[:I] for _ in range(8)])
    fd = mx_kscale(D)
    keysp = pack_weight(n((D, T)) / fd[:, None], "e2m1")
    notesp = pack_weight(n((D, U)) / fd[:, None], "e4m3")
    return {
        "query": (n((D, Q)) * 1.0 / np.sqrt(D) * fd[:, None]).astype(np.float32),
        "keys_words": keysp[0],
        "keys_scales": keysp[1],
        "notes_words": notesp[0],
        "notes_scales": notesp[1],
        "offs": striped8(idx),
        "offs2": striped8(idx2),
        "offs3": striped8(idx3),
        "offs4": striped8(idx4),
    }


def reference(query, keys_words, keys_scales, notes_words, notes_scales, offs, offs2, offs3, offs4):
    idx = unstriped8(offs)
    idx2 = unstriped8(offs2)
    idx3 = unstriped8(offs3)
    idx4 = unstriped8(offs4)
    keysu = unpack_weight(keys_words, keys_scales, "e2m1")
    notesu = unpack_weight(notes_words, notes_scales, "e4m3")
    queryq = mxq(f64(query), 0, "e4m3")
    a = queryq.T @ keysu
    b = queryq.T @ notesu
    w = np.concatenate([pick8(a, idx, 16), pick8(b, idx2, 16)], axis=1)
    f1 = np.zeros((Q, T))
    f1[np.arange(Q)[:, None], idx3[np.arange(Q) % 128 // 16]] = w
    cc = a - f1
    y = pick8(cc, idx4, 16) + w
    return y

@@ -1,0 +1,132 @@
+from contextlib import ExitStack
+
+import concourse.mybir as mybir
+
+D, T, U, I, J, Q = 512, 1024, 1024, 512, 256, 128
+FLOPS = 2 * D * Q * (T + U)
+
+F32 = mybir.dt.float32
+BF16 = mybir.dt.bfloat16
+I32 = mybir.dt.int32
+U32 = mybir.dt.uint32
+U16 = mybir.dt.uint16
+U8 = mybir.dt.uint8
+FP8X4 = mybir.dt.float8_e4m3fn_x4
+FP4X4 = mybir.dt.float4_e2m1fn_x4
+COPY = mybir.ActivationFunctionType.Copy
+ADD = mybir.AluOpType.add
+SUB = mybir.AluOpType.subtract
+
+P = 128
+PACK = 4
+N = 256
+GROUP = 16
+
+
+def load_scale_rows(nc, plane, scales):
+    for quadrant in range(4):
+        nc.sync.dma_start(
+            plane[32 * quadrant : 32 * quadrant + 4, :].bitcast(I32),
+            scales[0, 4 * quadrant : 4 * quadrant + 4, :].bitcast(I32),
+        )
+
+
+def tile_attend_joinedput_two_kernel(
+    tc, query, keys_words, keys_scales, notes_words, notes_scales, offs, offs2, offs3, offs4, out
+):
+    nc = tc.nc
+    with ExitStack() as ctx:
+        sb = ctx.enter_context(tc.tile_pool(name="sb", bufs=1))
+        psum = ctx.enter_context(tc.psum_pool(name="psum", bufs=1))
+
+        idx_a = sb.tile([P, J // GROUP], U16, name="idx_a")
+        idx_b = sb.tile([P, J // GROUP], U16, name="idx_b")
+        idx_put = sb.tile([P, I // GROUP], U16, name="idx_put")
+        idx_out = sb.tile([P, I // GROUP], U16, name="idx_out")
+
+        q_raw = sb.tile([P, PACK, Q], F32, name="q_raw", align_bytes=64)
+        q_bf = sb.tile([P, Q, PACK], BF16, name="q_bf", align_bytes=64)
+        q_codes = sb.tile([P, Q], U32, name="q_codes", align_bytes=64)
+        q_plane = sb.tile([P, Q], U8, name="q_plane", align_bytes=64)
+        k_codes = sb.tile([P, 2 * T], U8, name="k_codes", align_bytes=64)
+        k_plane = sb.tile([P, T], U8, name="k_plane", align_bytes=64)
+        n_codes = sb.tile([P, U], U32, name="n_codes", align_bytes=64)
+        n_plane = sb.tile([P, U], U8, name="n_plane", align_bytes=64)
+        a = sb.tile([P, T], F32, name="a", align_bytes=64)
+        b = sb.tile([P, U], F32, name="b", align_bytes=64)
+        w = sb.tile([P, I], F32, name="w", align_bytes=64)
+        f1 = sb.tile([P, T], F32, name="f1", align_bytes=64)
+        cc = sb.tile([P, T], F32, name="cc", align_bytes=64)
+        left = sb.tile([P, J], F32, name="left", align_bytes=64)
+        y_lo = sb.tile([P, J], F32, name="y_lo", align_bytes=64)
+        y_hi = sb.tile([P, J], F32, name="y_hi", align_bytes=64)
+
+        nc.vector.memset(k_plane[:].bitcast(I32), 0)
+        nc.vector.memset(n_plane[:].bitcast(I32), 0)
+        nc.vector.memset(f1[:], 0.0)
+
+        nc.sync.dma_start(q_raw[:], query.rearrange("(p t) q -> p t q", t=PACK))
+        load_scale_rows(nc, k_plane, keys_scales)
+        nc.sync.dma_start(k_codes[:].bitcast(I32), keys_words[0].bitcast(I32))
+        nc.sync.dma_start(
+            n_codes[:].bitcast(I32), notes_words[0].rearrange("p n t -> p (n t)").bitcast(I32)
+        )
+        nc.sync.dma_start(idx_a[:], offs)
+        load_scale_rows(nc, n_plane, notes_scales)
+        nc.sync.dma_start(idx_put[:], offs3)
+        nc.sync.dma_start(idx_b[:], offs2)
+        nc.sync.dma_start(idx_out[:], offs4)
+
+        half = Q // 2
+        src = q_raw[:].rearrange("p t (c i) -> p c t i", i=4)
+        dst = q_bf[:].rearrange("p (c i) t -> p c t i", i=4)
+        cut = half // 4
+        nc.vector.tensor_copy(dst[:, :cut], src[:, :cut])
+        nc.scalar.activation(dst[:, cut:], src[:, cut:], COPY)
+        nc.vector.quantize_mx(
+            out=q_codes[:].bitcast(FP8X4), scales=q_plane[:], in_=q_bf[:].rearrange("p q t -> p (q t)")
+        )
+
+        for j in range(T // N):
+            cols = slice(j * N, (j + 1) * N)
+            acc = psum.tile([P, N], F32, name="acc_a%d" % j)
+            nc.tensor.matmul_mx(
+                out=acc[:],
+                lhsT=q_codes[:].bitcast(FP8X4),
+                lhsT_scale=q_plane[:],
+                rhs=k_codes[:, 2 * j * N : 2 * (j + 1) * N].bitcast(FP4X4),
+                rhs_scale=k_plane[:, cols],
+                start=True,
+                stop=True,
+            )
+            if j % 2 == 0:
+                nc.vector.tensor_copy(a[:, cols], acc[:])
+            else:
+                nc.scalar.activation(a[:, cols], acc[:], COPY)
+        for j in range(U // N):
+            cols = slice(j * N, (j + 1) * N)
+            acc = psum.tile([P, N], F32, name="acc_b%d" % j)
+            nc.tensor.matmul_mx(
+                out=acc[:],
+                lhsT=q_codes[:].bitcast(FP8X4),
+                lhsT_scale=q_plane[:],
+                rhs=n_codes[:, cols].bitcast(FP8X4),
+                rhs_scale=n_plane[:, cols],
+                start=True,
+                stop=True,
+            )
+            nc.scalar.activation(b[:, cols], acc[:], COPY)
+
+        nc.vector.tensor_copy(w[:, :J], a[:].indirect(idx_a[:]))
+        nc.scalar.activation(w[:, J:], b[:].indirect(idx_b[:]), COPY)
+
+        k = J // GROUP
+        nc.vector.tensor_copy(f1[:].indirect(idx_put[:, :k]), w[:, :J])
+        nc.vector.tensor_copy(f1[:].indirect(idx_put[:, k:]), w[:, J:])
+        nc.vector.tensor_tensor(cc[:], a[:], f1[:], SUB)
+
+        nc.vector.tensor_tensor(y_lo[:], cc[:].indirect(idx_out[:, :k]), w[:, :J], ADD)
+        nc.scalar.activation(left[:], cc[:].indirect(idx_out[:, k:]), COPY)
+        nc.vector.tensor_tensor(y_hi[:], left[:], w[:, J:], ADD)
+        nc.sync.dma_start(out[:, :J], y_lo[:])
+        nc.sync.dma_start(out[:, J:], y_hi[:])

@@ -71,8 +71,8 @@ def tile_attend_joinedput_two_kernel(
         nc.sync.dma_start(
             n_codes[:].bitcast(I32), notes_words[0].rearrange("p n t -> p (n t)").bitcast(I32)
         )
-        nc.sync.dma_start(idx_a[:], offs)
         load_scale_rows(nc, n_plane, notes_scales)
+        nc.sync.dma_start(idx_a[:], offs)
         nc.sync.dma_start(idx_put[:], offs3)
         nc.sync.dma_start(idx_b[:], offs2)
         nc.sync.dma_start(idx_out[:], offs4)
@@ -80,32 +80,37 @@ def tile_attend_joinedput_two_kernel(
         half = Q // 2
         src = q_raw[:].rearrange("p t (c i) -> p c t i", i=4)
         dst = q_bf[:].rearrange("p (c i) t -> p c t i", i=4)
-        cut = half // 4
+        cut = 22
         nc.vector.tensor_copy(dst[:, :cut], src[:, :cut])
         nc.scalar.activation(dst[:, cut:], src[:, cut:], COPY)
         nc.vector.quantize_mx(
             out=q_codes[:].bitcast(FP8X4), scales=q_plane[:], in_=q_bf[:].rearrange("p q t -> p (q t)")
         )
 
-        for j in range(T // N):
-            cols = slice(j * N, (j + 1) * N)
-            acc = psum.tile([P, N], F32, name="acc_a%d" % j)
+        lo = 0
+        banks = []
+        for j, n in enumerate((256, 256, 256, 128, 128)):
+            cols = slice(lo, lo + n)
+            acc = psum.tile([P, n], F32, name="acc_a%d" % j, tag="bank%d" % j)
+            banks.append((cols, acc))
             nc.tensor.matmul_mx(
                 out=acc[:],
                 lhsT=q_codes[:].bitcast(FP8X4),
                 lhsT_scale=q_plane[:],
-                rhs=k_codes[:, 2 * j * N : 2 * (j + 1) * N].bitcast(FP4X4),
+                rhs=k_codes[:, 2 * lo : 2 * (lo + n)].bitcast(FP4X4),
                 rhs_scale=k_plane[:, cols],
                 start=True,
                 stop=True,
             )
-            if j % 2 == 0:
+            if j % 2 == 1:
                 nc.vector.tensor_copy(a[:, cols], acc[:])
             else:
                 nc.scalar.activation(a[:, cols], acc[:], COPY)
-        for j in range(U // N):
-            cols = slice(j * N, (j + 1) * N)
-            acc = psum.tile([P, N], F32, name="acc_b%d" % j)
+            lo = lo + n
+        lo = 0
+        for j, n in enumerate((256, 256, 256, 256)):
+            cols = slice(lo, lo + n)
+            acc = psum.tile([P, n], F32, name="acc_b%d" % j, tag="bank%d" % ((5 + j) % 8))
             nc.tensor.matmul_mx(
                 out=acc[:],
                 lhsT=q_codes[:].bitcast(FP8X4),
@@ -116,6 +121,7 @@ def tile_attend_joinedput_two_kernel(
                 stop=True,
             )
             nc.scalar.activation(b[:, cols], acc[:], COPY)
+            lo = lo + n
 
         nc.vector.tensor_copy(w[:, :J], a[:].indirect(idx_a[:]))
         nc.scalar.activation(w[:, J:], b[:].indirect(idx_b[:]), COPY)
@@ -123,7 +129,9 @@ def tile_attend_joinedput_two_kernel(
         k = J // GROUP
         nc.vector.tensor_copy(f1[:].indirect(idx_put[:, :k]), w[:, :J])
         nc.vector.tensor_copy(f1[:].indirect(idx_put[:, k:]), w[:, J:])
-        nc.vector.tensor_tensor(cc[:], a[:], f1[:], SUB)
+        nc.gpsimd.tensor_tensor(cc[:, :N], a[:, :N], f1[:, :N], SUB)
+        for cols, acc in banks[1:]:
+            nc.vector.tensor_tensor(cc[:, cols], acc[:], f1[:, cols], SUB)
 
         nc.vector.tensor_tensor(y_lo[:], cc[:].indirect(idx_out[:, :k]), w[:, :J], ADD)
         nc.scalar.activation(left[:], cc[:].indirect(idx_out[:, k:]), COPY)

@@ -23,9 +23,9 @@ N = 256
 GROUP = 16
 
 
-def load_scale_rows(nc, plane, scales):
-    for quadrant in range(4):
-        nc.sync.dma_start(
+def load_scale_rows(queue, plane, scales, quadrants):
+    for quadrant in quadrants:
+        queue.dma_start(
             plane[32 * quadrant : 32 * quadrant + 4, :].bitcast(I32),
             scales[0, 4 * quadrant : 4 * quadrant + 4, :].bitcast(I32),
         )
@@ -66,12 +66,13 @@ def tile_attend_joinedput_two_kernel(
         nc.vector.memset(f1[:], 0.0)
 
         nc.sync.dma_start(q_raw[:], query.rearrange("(p t) q -> p t q", t=PACK))
-        load_scale_rows(nc, k_plane, keys_scales)
+        load_scale_rows(nc.sync, k_plane, keys_scales, (0, 1, 2, 3))
         nc.sync.dma_start(k_codes[:].bitcast(I32), keys_words[0].bitcast(I32))
         nc.sync.dma_start(
             n_codes[:].bitcast(I32), notes_words[0].rearrange("p n t -> p (n t)").bitcast(I32)
         )
-        load_scale_rows(nc, n_plane, notes_scales)
+        load_scale_rows(nc.sync, n_plane, notes_scales, (0, 1))
+        load_scale_rows(nc.gpsimd, n_plane, notes_scales, (2, 3))
         nc.sync.dma_start(idx_a[:], offs)
         nc.sync.dma_start(idx_put[:], offs3)
         nc.sync.dma_start(idx_b[:], offs2)

from contextlib import ExitStack

import concourse.mybir as mybir

D, T, U, I, J, Q = 512, 1024, 1024, 512, 256, 128
FLOPS = 2 * D * Q * (T + U)

F32 = mybir.dt.float32
BF16 = mybir.dt.bfloat16
I32 = mybir.dt.int32
U32 = mybir.dt.uint32
U16 = mybir.dt.uint16
U8 = mybir.dt.uint8
FP8X4 = mybir.dt.float8_e4m3fn_x4
FP4X4 = mybir.dt.float4_e2m1fn_x4
COPY = mybir.ActivationFunctionType.Copy
ADD = mybir.AluOpType.add
SUB = mybir.AluOpType.subtract

P = 128
PACK = 4
N = 256
GROUP = 16


def load_scale_rows(queue, plane, scales, quadrants):
    for quadrant in quadrants:
        queue.dma_start(
            plane[32 * quadrant : 32 * quadrant + 4, :].bitcast(I32),
            scales[0, 4 * quadrant : 4 * quadrant + 4, :].bitcast(I32),
        )


def tile_attend_joinedput_two_kernel(
    tc, query, keys_words, keys_scales, notes_words, notes_scales, offs, offs2, offs3, offs4, out
):
    nc = tc.nc
    with ExitStack() as ctx:
        sb = ctx.enter_context(tc.tile_pool(name="sb", bufs=1))
        psum = ctx.enter_context(tc.psum_pool(name="psum", bufs=1))

        idx_a = sb.tile([P, J // GROUP], U16, name="idx_a")
        idx_b = sb.tile([P, J // GROUP], U16, name="idx_b")
        idx_put = sb.tile([P, I // GROUP], U16, name="idx_put")
        idx_out = sb.tile([P, I // GROUP], U16, name="idx_out")

        q_raw = sb.tile([P, PACK, Q], F32, name="q_raw", align_bytes=64)
        q_bf = sb.tile([P, Q, PACK], BF16, name="q_bf", align_bytes=64)
        q_codes = sb.tile([P, Q], U32, name="q_codes", align_bytes=64)
        q_plane = sb.tile([P, Q], U8, name="q_plane", align_bytes=64)
        k_codes = sb.tile([P, 2 * T], U8, name="k_codes", align_bytes=64)
        k_plane = sb.tile([P, T], U8, name="k_plane", align_bytes=64)
        n_codes = sb.tile([P, U], U32, name="n_codes", align_bytes=64)
        n_plane = sb.tile([P, U], U8, name="n_plane", align_bytes=64)
        a = sb.tile([P, T], F32, name="a", align_bytes=64)
        b = sb.tile([P, U], F32, name="b", align_bytes=64)
        w = sb.tile([P, I], F32, name="w", align_bytes=64)
        f1 = sb.tile([P, T], F32, name="f1", align_bytes=64)
        cc = sb.tile([P, T], F32, name="cc", align_bytes=64)
        left = sb.tile([P, J], F32, name="left", align_bytes=64)
        y_lo = sb.tile([P, J], F32, name="y_lo", align_bytes=64)
        y_hi = sb.tile([P, J], F32, name="y_hi", align_bytes=64)

        nc.vector.memset(k_plane[:].bitcast(I32), 0)
        nc.vector.memset(n_plane[:].bitcast(I32), 0)
        nc.vector.memset(f1[:], 0.0)

        nc.sync.dma_start(q_raw[:], query.rearrange("(p t) q -> p t q", t=PACK))
        load_scale_rows(nc.sync, k_plane, keys_scales, (0, 1, 2, 3))
        nc.sync.dma_start(k_codes[:].bitcast(I32), keys_words[0].bitcast(I32))
        nc.sync.dma_start(
            n_codes[:].bitcast(I32), notes_words[0].rearrange("p n t -> p (n t)").bitcast(I32)
        )
        load_scale_rows(nc.sync, n_plane, notes_scales, (0, 1))
        load_scale_rows(nc.gpsimd, n_plane, notes_scales, (2, 3))
        nc.sync.dma_start(idx_a[:], offs)
        nc.sync.dma_start(idx_put[:], offs3)
        nc.sync.dma_start(idx_b[:], offs2)
        nc.sync.dma_start(idx_out[:], offs4)

        half = Q // 2
        src = q_raw[:].rearrange("p t (c i) -> p c t i", i=4)
        dst = q_bf[:].rearrange("p (c i) t -> p c t i", i=4)
        cut = 22
        nc.vector.tensor_copy(dst[:, :cut], src[:, :cut])
        nc.scalar.activation(dst[:, cut:], src[:, cut:], COPY)
        nc.vector.quantize_mx(
            out=q_codes[:].bitcast(FP8X4), scales=q_plane[:], in_=q_bf[:].rearrange("p q t -> p (q t)")
        )

        lo = 0
        banks = []
        for j, n in enumerate((256, 256, 256, 128, 128)):
            cols = slice(lo, lo + n)
            acc = psum.tile([P, n], F32, name="acc_a%d" % j, tag="bank%d" % j)
            banks.append((cols, acc))
            nc.tensor.matmul_mx(
                out=acc[:],
                lhsT=q_codes[:].bitcast(FP8X4),
                lhsT_scale=q_plane[:],
                rhs=k_codes[:, 2 * lo : 2 * (lo + n)].bitcast(FP4X4),
                rhs_scale=k_plane[:, cols],
                start=True,
                stop=True,
            )
            if j % 2 == 1:
                nc.vector.tensor_copy(a[:, cols], acc[:])
            else:
                nc.scalar.activation(a[:, cols], acc[:], COPY)
            lo = lo + n
        lo = 0
        for j, n in enumerate((256, 256, 256, 256)):
            cols = slice(lo, lo + n)
            acc = psum.tile([P, n], F32, name="acc_b%d" % j, tag="bank%d" % ((5 + j) % 8))
            nc.tensor.matmul_mx(
                out=acc[:],
                lhsT=q_codes[:].bitcast(FP8X4),
                lhsT_scale=q_plane[:],
                rhs=n_codes[:, cols].bitcast(FP8X4),
                rhs_scale=n_plane[:, cols],
                start=True,
                stop=True,
            )
            nc.scalar.activation(b[:, cols], acc[:], COPY)
            lo = lo + n

        nc.vector.tensor_copy(w[:, :J], a[:].indirect(idx_a[:]))
        nc.scalar.activation(w[:, J:], b[:].indirect(idx_b[:]), COPY)

        k = J // GROUP
        nc.vector.tensor_copy(f1[:].indirect(idx_put[:, :k]), w[:, :J])
        nc.vector.tensor_copy(f1[:].indirect(idx_put[:, k:]), w[:, J:])
        nc.gpsimd.tensor_tensor(cc[:, :N], a[:, :N], f1[:, :N], SUB)
        for cols, acc in banks[1:]:
            nc.vector.tensor_tensor(cc[:, cols], acc[:], f1[:, cols], SUB)

        nc.vector.tensor_tensor(y_lo[:], cc[:].indirect(idx_out[:, :k]), w[:, :J], ADD)
        nc.scalar.activation(left[:], cc[:].indirect(idx_out[:, k:]), COPY)
        nc.vector.tensor_tensor(y_hi[:], left[:], w[:, J:], ADD)
        nc.sync.dma_start(out[:, :J], y_lo[:])
        nc.sync.dma_start(out[:, J:], y_hi[:])
